import numpy as np
import ml_dtypes


def mxq(x, axis, fmt="e4m3"):
    dtype, down = {"e4m3": (ml_dtypes.float8_e4m3fn, 7), "e5m2": (ml_dtypes.float8_e5m2, 14)}[fmt]
    v = np.moveaxis(np.asarray(x, np.float32).astype(ml_dtypes.bfloat16).astype(np.float64), axis, -1)
    blocks = v.reshape(v.shape[:-1] + (-1, 32))
    amax = np.abs(blocks).max(-1, keepdims=True)
    byte = np.maximum(np.where(amax > 0, np.frexp(amax)[1] - 1 + 127, 0) - down, 1)
    scale = np.exp2(byte - 127.0)
    codes = (blocks / scale).astype(np.float32).astype(dtype).astype(np.float64)
    return np.moveaxis((codes * scale).reshape(v.shape), -1, axis)


WIDE = False


def mx_kscale(k):
    if not WIDE:
        return np.ones(k)
    levels = np.array([10, -10, 5, -5, 0])
    if k % 512:
        return np.exp2(np.random.permutation(np.resize(levels, k // 32))).repeat(32)
    a = np.empty((k // 512, 16))
    for p in range(k // 512):
        a[p, :8] = np.random.permutation(np.resize(levels, 8))
        for g in range(8):
            far = levels[np.abs(levels - a[p, g]) >= 10]
            a[p, g + 8] = far[np.random.randint(len(far))]
    return np.exp2(a.ravel()).repeat(32)


def f64(x):
    return np.asarray(x).astype(np.float64)


def striped(idx):
    return np.tile(np.asarray(idx).reshape(-1, 16).T, (8, 1)).astype(np.uint16)


def unstriped(offs):
    return offs[:16].T.reshape(-1).astype(np.int64)


E2M1 = np.array([0.0, 0.5, 1.0, 1.5, 2.0, 3.0, 4.0, 6.0, -0.0, -0.5, -1.0, -1.5, -2.0, -3.0, -4.0, -6.0])


def pack_weight(w, fmt):
    k, n = w.shape
    w = f64(np.asarray(w, np.float32).astype(ml_dtypes.bfloat16)).reshape(k // 32, 32, n)
    amax = np.abs(w).max(1)
    if fmt == "e4m3":
        byte = np.frexp(amax)[1] - 1 + 127 - 7
    else:
        mant, ex = np.frexp(amax / 6.0)
        byte = np.where(mant > 0.5, ex, ex - 1) + 127
    byte = np.clip(np.where(amax > 0, byte, 1), 1, 254)
    scaled = (w * np.exp2(127.0 - byte)[:, None, :]).reshape(k, n).astype(np.float32)
    by_word = np.ascontiguousarray(scaled.reshape(k // 512, 128, 4, n).transpose(0, 1, 3, 2))
    if fmt == "e4m3":
        words = by_word.astype(ml_dtypes.float8_e4m3fn).view(np.uint8)
    else:
        c = by_word.astype(ml_dtypes.float4_e2m1fn).view(np.uint8) & 0xF
        words = (c[..., 0::2] | (c[..., 1::2] << 4)).reshape(k // 512, 128, 2 * n)
    return np.ascontiguousarray(words), np.ascontiguousarray(byte.astype(np.uint8).reshape(k // 512, 16, n))


def unpack_weight(words, scales, fmt):
    g, _, n = scales.shape
    words = np.ascontiguousarray(words).reshape(g, 128, n, -1)
    if fmt == "e4m3":
        vals = words.view(ml_dtypes.float8_e4m3fn).astype(np.float64)
    else:
        nib = np.empty((g, 128, n, 4), np.uint8)
        nib[..., 0::2] = words & 0xF
        nib[..., 1::2] = words >> 4
        vals = E2M1[nib]
    vals = vals * np.repeat(np.exp2(scales.astype(np.float64) - 127.0), 8, axis=1)[..., None]
    return vals.transpose(0, 1, 3, 2).reshape(g * 512, n)


def sigmoid(v):
    return 1.0 / (1.0 + np.exp(-v))


K, R, F, T, J, G = 512, 128, 512, 2048, 512, 64


def setup_inputs():
    n = np.random.standard_normal
    idx = np.random.permutation(T)[:J]
    fk = mx_kscale(K)
    dtabp = pack_weight(n((K, T)) / fk[:, None], "e2m1")
    tabp = pack_weight(n((K, T)) / fk[:, None], "e2m1")
    return {
        "dtab_words": dtabp[0],
        "dtab_scales": dtabp[1],
        "tab_words": tabp[0],
        "tab_scales": tabp[1],
        "w1": (n((K, R)) * 1 / np.sqrt(K) * fk[:, None]).astype(np.float32),
        "steep": (np.random.uniform(1.0, 4.0, (R, 1))).astype(np.float32),
        "og": (np.random.uniform(0.5, 2.0, (R, 1))).astype(np.float32),
        "base": (0.3 * n((R, G))).astype(np.float32),
        "offs": striped(idx),
    }


def reference(dtab_words, dtab_scales, tab_words, tab_scales, w1, steep, og, base, offs):
    idx = unstriped(offs)
    dtabu = unpack_weight(dtab_words, dtab_scales, "e2m1")
    tabu = unpack_weight(tab_words, tab_scales, "e2m1")
    w1q = mxq(f64(w1), 0, "e4m3")
    tabidxg = tabu[:, idx]
    a = w1q.T @ tabidxg
    dtabidxg = dtabu[:, idx]
    ta = w1q.T @ dtabidxg
    h1 = np.tanh(a)
    p = sigmoid(a * f64(steep))
    z = p.reshape(R, G, J // G).sum(axis=2)
    th1 = ta * (1.0 - np.square(h1))
    tp = ta * f64(steep) * p * (1.0 - p)
    tz = tp.reshape(R, G, J // G).sum(axis=2)
    tu1 = ((tp * h1 + th1 * p).reshape(R, G, J // G).sum(axis=2) - tz * (p * h1).reshape(R, G, J // G).sum(axis=2) / z) / z
    y = tu1 * f64(og) + f64(base)
    return y

@@ -1,0 +1,129 @@
+from contextlib import ExitStack
+
+import concourse.mybir as mybir
+
+K, R, T, J, G = 512, 128, 2048, 512, 64
+GROUP = J // G
+P = 128
+PACK = 4
+HALVES = 2
+
+F32 = mybir.dt.float32
+BF16 = mybir.dt.bfloat16
+I32 = mybir.dt.int32
+U32 = mybir.dt.uint32
+U16 = mybir.dt.uint16
+U8 = mybir.dt.uint8
+E4M3X4 = mybir.dt.float8_e4m3fn_x4
+E2M1X4 = mybir.dt.float4_e2m1fn_x4
+ALU = mybir.AluOpType
+ACT = mybir.ActivationFunctionType
+AXIS = mybir.AxisListType
+
+FLOPS = 2 * 2 * K * R * J
+
+
+def grouped(ap):
+    return ap.rearrange("p (g i) -> p g i", i=GROUP)
+
+
+def tile_attend_tgroupvote_kernel(tc, dtab_words, dtab_scales, tab_words, tab_scales, w1, steep, og, base, offs, out):
+    nc = tc.nc
+    with ExitStack() as ctx:
+        sb = ctx.enter_context(tc.tile_pool(name="sb", bufs=1))
+        ps = ctx.enter_context(tc.psum_pool(name="ps", bufs=1))
+
+        offsets = sb.tile([P, J // 16], U16, name="offsets")
+        tab_w = sb.tile([P, T], U16, name="tab_w")
+        dtab_w = sb.tile([P, T], U16, name="dtab_w")
+        tab_s = sb.tile([P, T], U8, name="tab_s")
+        dtab_s = sb.tile([P, T], U8, name="dtab_s")
+        w_raw = sb.tile([P, PACK, R], F32, name="w_raw")
+        steep_c = sb.tile([P, 1], F32, name="steep_c")
+        og_c = sb.tile([P, 1], F32, name="og_c")
+        base_t = sb.tile([P, G], F32, name="base_t")
+
+        nc.vector.memset(tab_s[:].bitcast(I32), 0)
+        nc.vector.memset(dtab_s[:].bitcast(I32), 0)
+
+        nc.sync.dma_start(offsets[:], offs)
+        nc.scalar.dma_start(w_raw[:], w1.rearrange("(p t) r -> p t r", t=PACK))
+        for q in range(4):
+            nc.sync.dma_start(tab_s[32 * q : 32 * q + 4, :].bitcast(I32), tab_scales[0, 4 * q : 4 * q + 4, :].bitcast(I32))
+        nc.sync.dma_start(tab_w[:].bitcast(I32), tab_words[0].bitcast(I32))
+        nc.sync.dma_start(dtab_w[:].bitcast(I32), dtab_words[0].bitcast(I32))
+        for q in range(4):
+            nc.sync.dma_start(dtab_s[32 * q : 32 * q + 4, :].bitcast(I32), dtab_scales[0, 4 * q : 4 * q + 4, :].bitcast(I32))
+        nc.gpsimd.dma_start(steep_c[:], steep)
+        nc.gpsimd.dma_start(og_c[:], og)
+        nc.gpsimd.dma_start(base_t[:], base)
+
+        w_bf = sb.tile([P, R, PACK], BF16, name="w_bf", align_bytes=64)
+        w_codes = sb.tile([P, R], U32, name="w_codes", align_bytes=64)
+        w_scales = sb.tile([P, R], U8, name="w_scales", align_bytes=64)
+        tab_wg = sb.tile([P, J], U16, name="tab_wg", align_bytes=64)
+        tab_sg = sb.tile([P, J], U8, name="tab_sg", align_bytes=64)
+        dtab_wg = sb.tile([P, J], U16, name="dtab_wg", align_bytes=64)
+        dtab_sg = sb.tile([P, J], U8, name="dtab_sg", align_bytes=64)
+
+        nc.vector.tensor_copy(w_bf[:], w_raw[:].rearrange("p t r -> p r t"))
+        nc.vector.tensor_copy(tab_sg[:], tab_s[:].indirect(offsets[:]))
+        nc.vector.quantize_mx(out=w_codes[:].bitcast(E4M3X4), scales=w_scales[:], in_=w_bf[:].rearrange("p r t -> p (r t)"))
+        nc.vector.tensor_copy(tab_wg[:], tab_w[:].indirect(offsets[:]))
+        a = ps.tile([P, J], F32, name="a")
+        nc.tensor.matmul_mx(out=a[:], lhsT=w_codes[:].bitcast(E4M3X4), lhsT_scale=w_scales[:],
+                            rhs=tab_wg[:].bitcast(E2M1X4), rhs_scale=tab_sg[:], start=True, stop=True)
+        nc.vector.tensor_copy(dtab_wg[:], dtab_w[:].indirect(offsets[:]))
+        nc.vector.tensor_copy(dtab_sg[:], dtab_s[:].indirect(offsets[:]))
+        ta = ps.tile([P, J], F32, name="ta")
+        nc.tensor.matmul_mx(out=ta[:], lhsT=w_codes[:].bitcast(E4M3X4), lhsT_scale=w_scales[:],
+                            rhs=dtab_wg[:].bitcast(E2M1X4), rhs_scale=dtab_sg[:], start=True, stop=True)
+
+        pp = sb.tile([P, 2, J], F32, name="pp")
+        p = pp[:, 0, :]
+        ph = pp[:, 1, :]
+        h = sb.tile([P, J], F32, name="h")
+        hsq = sb.tile([P, J], F32, name="hsq")
+        nc.scalar.activation(p, a[:], ACT.Sigmoid, scale=steep_c[:])
+        nc.scalar.activation(h[:], a[:], ACT.Tanh)
+        nc.scalar.activation(hsq[:], h[:], ACT.Square)
+
+        z = sb.tile([P, G], F32, name="z")
+        s2 = sb.tile([P, G], F32, name="s2")
+        rz = sb.tile([P, G], F32, name="rz")
+        m = sb.tile([P, G], F32, name="m")
+        gain = sb.tile([P, G], F32, name="gain")
+        pt = sb.tile([P, J], F32, name="pt")
+        nc.vector.tensor_tensor(ph, p, h[:], ALU.mult)
+        nc.vector.tensor_reduce(z[:], grouped(p), AXIS.X, ALU.add)
+        nc.vector.tensor_reduce(s2[:], grouped(ph), AXIS.X, ALU.add)
+        nc.vector.reciprocal(rz[:], z[:])
+        nc.vector.tensor_tensor(pt[:], ta[:], p, ALU.mult)
+        nc.vector.tensor_tensor(m[:], s2[:], rz[:], ALU.mult)
+        nc.vector.tensor_scalar(gain[:], rz[:], og_c[:], -1.0, ALU.mult, ALU.mult)
+
+        JH, GH = J // HALVES, G // HALVES
+        cols = [slice(i * JH, (i + 1) * JH) for i in range(HALVES)]
+        gs = [slice(i * GH, (i + 1) * GH) for i in range(HALVES)]
+        d = [sb.tile([P, JH], F32, name=f"d{i}") for i in range(HALVES)]
+        e = [sb.tile([P, JH], F32, name=f"e{i}") for i in range(HALVES)]
+        f = [sb.tile([P, JH], F32, name=f"f{i}") for i in range(HALVES)]
+        t = [sb.tile([P, JH], F32, name=f"t{i}") for i in range(HALVES)]
+        r = [sb.tile([P, GH], F32, name=f"r{i}") for i in range(HALVES)]
+        y0 = [sb.tile([P, GH], F32, name=f"y0{i}") for i in range(HALVES)]
+        y = sb.tile([P, G], F32, name="y")
+        for i in range(HALVES):
+            nc.vector.tensor_tensor(grouped(d[i][:]), grouped(h[:, cols[i]]), m[:, gs[i]].unsqueeze(2).to_broadcast([P, GH, GROUP]), ALU.subtract)
+        for i in range(HALVES):
+            nc.vector.scalar_tensor_tensor(e[i][:], pp[:, 0, cols[i]], 1.0, d[i][:], ALU.subtract, ALU.mult)
+        for i in range(HALVES):
+            nc.vector.scalar_tensor_tensor(f[i][:], e[i][:], steep_c[:], hsq[:, cols[i]], ALU.mult, ALU.add)
+        for i in range(HALVES):
+            nc.vector.scalar_tensor_tensor(t[i][:], f[i][:], 1.0, pt[:, cols[i]], ALU.subtract, ALU.mult)
+        for i in range(HALVES):
+            nc.vector.tensor_reduce(r[i][:], grouped(t[i][:]), AXIS.X, ALU.add)
+        for i in range(HALVES):
+            nc.vector.tensor_tensor(y0[i][:], r[i][:], gain[:, gs[i]], ALU.mult)
+        for i in range(HALVES):
+            nc.vector.tensor_tensor(y[:, gs[i]], y0[i][:], base_t[:, gs[i]], ALU.add)
+        nc.sync.dma_start(out, y[:])

@@ -35,10 +35,9 @@ def tile_attend_tgroupvote_kernel(tc, dtab_words, dtab_scales, tab_words, tab_sc
 
         offsets = sb.tile([P, J // 16], U16, name="offsets")
         tab_w = sb.tile([P, T], U16, name="tab_w")
-        dtab_w = sb.tile([P, T], U16, name="dtab_w")
         tab_s = sb.tile([P, T], U8, name="tab_s")
-        dtab_s = sb.tile([P, T], U8, name="dtab_s")
-        w_raw = sb.tile([P, PACK, R], F32, name="w_raw")
+        dtab_s = sb.tile([P, T], U8, name="dtab_s", tag="b", align_bytes=64)
+        w_raw = sb.tile([P, PACK, R], F32, name="w_raw", tag="a", align_bytes=64)
         steep_c = sb.tile([P, 1], F32, name="steep_c")
         og_c = sb.tile([P, 1], F32, name="og_c")
         base_t = sb.tile([P, G], F32, name="base_t")
@@ -48,13 +47,12 @@ def tile_attend_tgroupvote_kernel(tc, dtab_words, dtab_scales, tab_words, tab_sc
 
         nc.sync.dma_start(offsets[:], offs)
         nc.scalar.dma_start(w_raw[:], w1.rearrange("(p t) r -> p t r", t=PACK))
+        nc.sync.dma_start(steep_c[:], steep)
+        nc.scalar.dma_start(tab_w[:].bitcast(I32), tab_words[0].bitcast(I32))
         for q in range(4):
             nc.sync.dma_start(tab_s[32 * q : 32 * q + 4, :].bitcast(I32), tab_scales[0, 4 * q : 4 * q + 4, :].bitcast(I32))
-        nc.sync.dma_start(tab_w[:].bitcast(I32), tab_words[0].bitcast(I32))
-        nc.sync.dma_start(dtab_w[:].bitcast(I32), dtab_words[0].bitcast(I32))
         for q in range(4):
             nc.sync.dma_start(dtab_s[32 * q : 32 * q + 4, :].bitcast(I32), dtab_scales[0, 4 * q : 4 * q + 4, :].bitcast(I32))
-        nc.gpsimd.dma_start(steep_c[:], steep)
         nc.gpsimd.dma_start(og_c[:], og)
         nc.gpsimd.dma_start(base_t[:], base)
 
@@ -63,48 +61,43 @@ def tile_attend_tgroupvote_kernel(tc, dtab_words, dtab_scales, tab_words, tab_sc
         w_scales = sb.tile([P, R], U8, name="w_scales", align_bytes=64)
         tab_wg = sb.tile([P, J], U16, name="tab_wg", align_bytes=64)
         tab_sg = sb.tile([P, J], U8, name="tab_sg", align_bytes=64)
-        dtab_wg = sb.tile([P, J], U16, name="dtab_wg", align_bytes=64)
-        dtab_sg = sb.tile([P, J], U8, name="dtab_sg", align_bytes=64)
 
         nc.vector.tensor_copy(w_bf[:], w_raw[:].rearrange("p t r -> p r t"))
+        dtab_w = sb.tile([P, T], U16, name="dtab_w", tag="a", align_bytes=64)
+        nc.scalar.dma_start(dtab_w[:].bitcast(I32), dtab_words[0].bitcast(I32))
         nc.vector.tensor_copy(tab_sg[:], tab_s[:].indirect(offsets[:]))
         nc.vector.quantize_mx(out=w_codes[:].bitcast(E4M3X4), scales=w_scales[:], in_=w_bf[:].rearrange("p r t -> p (r t)"))
         nc.vector.tensor_copy(tab_wg[:], tab_w[:].indirect(offsets[:]))
         a = ps.tile([P, J], F32, name="a")
         nc.tensor.matmul_mx(out=a[:], lhsT=w_codes[:].bitcast(E4M3X4), lhsT_scale=w_scales[:],
                             rhs=tab_wg[:].bitcast(E2M1X4), rhs_scale=tab_sg[:], start=True, stop=True)
-        nc.vector.tensor_copy(dtab_wg[:], dtab_w[:].indirect(offsets[:]))
+        dtab_sg = sb.tile([P, J], U8, name="dtab_sg", align_bytes=64)
         nc.vector.tensor_copy(dtab_sg[:], dtab_s[:].indirect(offsets[:]))
+        dtab_wg = sb.tile([P, J], U16, name="dtab_wg", align_bytes=64)
+        nc.vector.tensor_copy(dtab_wg[:], dtab_w[:].indirect(offsets[:]))
         ta = ps.tile([P, J], F32, name="ta")
         nc.tensor.matmul_mx(out=ta[:], lhsT=w_codes[:].bitcast(E4M3X4), lhsT_scale=w_scales[:],
                             rhs=dtab_wg[:].bitcast(E2M1X4), rhs_scale=dtab_sg[:], start=True, stop=True)
 
-        pp = sb.tile([P, 2, J], F32, name="pp")
-        p = pp[:, 0, :]
-        ph = pp[:, 1, :]
+        pp = sb.tile([P, J], F32, name="pp")
+        p = pp[:]
+        ph_t = sb.tile([P, J], F32, name="ph_t", tag="a", align_bytes=64)
+        z_t = sb.tile([P, G], F32, name="z_t", tag="b", align_bytes=64)
+        ph = ph_t[:]
+        z = z_t[:]
         h = sb.tile([P, J], F32, name="h")
         hsq = sb.tile([P, J], F32, name="hsq")
         nc.scalar.activation(p, a[:], ACT.Sigmoid, scale=steep_c[:])
         nc.scalar.activation(h[:], a[:], ACT.Tanh)
         nc.scalar.activation(hsq[:], h[:], ACT.Square)
 
-        z = sb.tile([P, G], F32, name="z")
         s2 = sb.tile([P, G], F32, name="s2")
         rz = sb.tile([P, G], F32, name="rz")
         m = sb.tile([P, G], F32, name="m")
-        gain = sb.tile([P, G], F32, name="gain")
-        pt = sb.tile([P, J], F32, name="pt")
-        nc.vector.tensor_tensor(ph, p, h[:], ALU.mult)
-        nc.vector.tensor_reduce(z[:], grouped(p), AXIS.X, ALU.add)
-        nc.vector.tensor_reduce(s2[:], grouped(ph), AXIS.X, ALU.add)
-        nc.vector.reciprocal(rz[:], z[:])
-        nc.vector.tensor_tensor(pt[:], ta[:], p, ALU.mult)
-        nc.vector.tensor_tensor(m[:], s2[:], rz[:], ALU.mult)
-        nc.vector.tensor_scalar(gain[:], rz[:], og_c[:], -1.0, ALU.mult, ALU.mult)
-
         JH, GH = J // HALVES, G // HALVES
         cols = [slice(i * JH, (i + 1) * JH) for i in range(HALVES)]
         gs = [slice(i * GH, (i + 1) * GH) for i in range(HALVES)]
+        pt = [sb.tile([P, JH], F32, name=f"pt{i}") for i in range(HALVES)]
         d = [sb.tile([P, JH], F32, name=f"d{i}") for i in range(HALVES)]
         e = [sb.tile([P, JH], F32, name=f"e{i}") for i in range(HALVES)]
         f = [sb.tile([P, JH], F32, name=f"f{i}") for i in range(HALVES)]
@@ -112,18 +105,25 @@ def tile_attend_tgroupvote_kernel(tc, dtab_words, dtab_scales, tab_words, tab_sc
         r = [sb.tile([P, GH], F32, name=f"r{i}") for i in range(HALVES)]
         y0 = [sb.tile([P, GH], F32, name=f"y0{i}") for i in range(HALVES)]
         y = sb.tile([P, G], F32, name="y")
+        nc.vector.tensor_reduce(z, grouped(p), AXIS.X, ALU.add)
+        nc.vector.tensor_tensor(ph, p, h[:], ALU.mult)
+        nc.vector.reciprocal(rz[:], z)
+        nc.vector.tensor_reduce(s2[:], grouped(ph), AXIS.X, ALU.add)
+        nc.vector.tensor_tensor(pt[0][:], ta[:, cols[0]], pp[:, cols[0]], ALU.mult)
+        nc.vector.tensor_tensor(m[:], s2[:], rz[:], ALU.mult)
+        nc.vector.tensor_tensor(pt[1][:], ta[:, cols[1]], pp[:, cols[1]], ALU.mult)
         for i in range(HALVES):
             nc.vector.tensor_tensor(grouped(d[i][:]), grouped(h[:, cols[i]]), m[:, gs[i]].unsqueeze(2).to_broadcast([P, GH, GROUP]), ALU.subtract)
         for i in range(HALVES):
-            nc.vector.scalar_tensor_tensor(e[i][:], pp[:, 0, cols[i]], 1.0, d[i][:], ALU.subtract, ALU.mult)
+            nc.vector.scalar_tensor_tensor(e[i][:], pp[:, cols[i]], 1.0, d[i][:], ALU.subtract, ALU.mult)
         for i in range(HALVES):
             nc.vector.scalar_tensor_tensor(f[i][:], e[i][:], steep_c[:], hsq[:, cols[i]], ALU.mult, ALU.add)
         for i in range(HALVES):
-            nc.vector.scalar_tensor_tensor(t[i][:], f[i][:], 1.0, pt[:, cols[i]], ALU.subtract, ALU.mult)
+            nc.vector.scalar_tensor_tensor(t[i][:], f[i][:], 1.0, pt[i][:], ALU.subtract, ALU.mult)
         for i in range(HALVES):
             nc.vector.tensor_reduce(r[i][:], grouped(t[i][:]), AXIS.X, ALU.add)
         for i in range(HALVES):
-            nc.vector.tensor_tensor(y0[i][:], r[i][:], gain[:, gs[i]], ALU.mult)
+            nc.vector.scalar_tensor_tensor(y0[i][:], r[i][:], og_c[:], rz[:, gs[i]], ALU.mult, ALU.mult)
         for i in range(HALVES):
-            nc.vector.tensor_tensor(y[:, gs[i]], y0[i][:], base_t[:, gs[i]], ALU.add)
+            nc.vector.tensor_tensor(y[:, gs[i]], base_t[:, gs[i]], y0[i][:], ALU.subtract)
         nc.sync.dma_start(out, y[:])

@@ -37,66 +37,65 @@ def tile_attend_tgroupvote_kernel(tc, dtab_words, dtab_scales, tab_words, tab_sc
         tab_w = sb.tile([P, T], U16, name="tab_w")
         tab_s = sb.tile([P, T], U8, name="tab_s")
         dtab_s = sb.tile([P, T], U8, name="dtab_s", tag="b", align_bytes=64)
-        w_raw = sb.tile([P, PACK, R], F32, name="w_raw", tag="a", align_bytes=64)
+        w_raw = sb.tile([P, PACK, R], F32, name="w_raw")
+        dtab_w = sb.tile([P, T], U16, name="dtab_w", tag="a", align_bytes=64)
         steep_c = sb.tile([P, 1], F32, name="steep_c")
-        og_c = sb.tile([P, 1], F32, name="og_c")
-        base_t = sb.tile([P, G], F32, name="base_t")
 
         nc.vector.memset(tab_s[:].bitcast(I32), 0)
         nc.vector.memset(dtab_s[:].bitcast(I32), 0)
 
+        nc.sync.dma_start(w_raw[:], w1.rearrange("(p t) r -> p t r", t=PACK))
         nc.sync.dma_start(offsets[:], offs)
-        nc.scalar.dma_start(w_raw[:], w1.rearrange("(p t) r -> p t r", t=PACK))
-        nc.sync.dma_start(steep_c[:], steep)
-        nc.scalar.dma_start(tab_w[:].bitcast(I32), tab_words[0].bitcast(I32))
+        nc.scalar.dma_start(steep_c[:], steep)
         for q in range(4):
             nc.sync.dma_start(tab_s[32 * q : 32 * q + 4, :].bitcast(I32), tab_scales[0, 4 * q : 4 * q + 4, :].bitcast(I32))
+        nc.sync.dma_start(tab_w[:].bitcast(I32), tab_words[0].bitcast(I32))
         for q in range(4):
             nc.sync.dma_start(dtab_s[32 * q : 32 * q + 4, :].bitcast(I32), dtab_scales[0, 4 * q : 4 * q + 4, :].bitcast(I32))
-        nc.gpsimd.dma_start(og_c[:], og)
-        nc.gpsimd.dma_start(base_t[:], base)
+        nc.sync.dma_start(dtab_w[:].bitcast(I32), dtab_words[0].bitcast(I32))
 
         w_bf = sb.tile([P, R, PACK], BF16, name="w_bf", align_bytes=64)
         w_codes = sb.tile([P, R], U32, name="w_codes", align_bytes=64)
         w_scales = sb.tile([P, R], U8, name="w_scales", align_bytes=64)
-        tab_wg = sb.tile([P, J], U16, name="tab_wg", align_bytes=64)
+        tab_wg = [sb.tile([P, J // HALVES], U16, name=f"tab_wg{i}", align_bytes=64) for i in range(HALVES)]
         tab_sg = sb.tile([P, J], U8, name="tab_sg", align_bytes=64)
 
         nc.vector.tensor_copy(w_bf[:], w_raw[:].rearrange("p t r -> p r t"))
-        dtab_w = sb.tile([P, T], U16, name="dtab_w", tag="a", align_bytes=64)
-        nc.scalar.dma_start(dtab_w[:].bitcast(I32), dtab_words[0].bitcast(I32))
         nc.vector.tensor_copy(tab_sg[:], tab_s[:].indirect(offsets[:]))
         nc.vector.quantize_mx(out=w_codes[:].bitcast(E4M3X4), scales=w_scales[:], in_=w_bf[:].rearrange("p r t -> p (r t)"))
-        nc.vector.tensor_copy(tab_wg[:], tab_w[:].indirect(offsets[:]))
-        a = ps.tile([P, J], F32, name="a")
-        nc.tensor.matmul_mx(out=a[:], lhsT=w_codes[:].bitcast(E4M3X4), lhsT_scale=w_scales[:],
-                            rhs=tab_wg[:].bitcast(E2M1X4), rhs_scale=tab_sg[:], start=True, stop=True)
+        JH, GH = J // HALVES, G // HALVES
+        cols = [slice(i * JH, (i + 1) * JH) for i in range(HALVES)]
+        gs = [slice(i * GH, (i + 1) * GH) for i in range(HALVES)]
+        a = [ps.tile([P, JH], F32, name=f"a{i}") for i in range(HALVES)]
+        for i in range(HALVES):
+            nc.vector.tensor_copy(tab_wg[i][:], tab_w[:].indirect(offsets[:, i * JH // 16 : (i + 1) * JH // 16]))
+            nc.tensor.matmul_mx(out=a[i][:], lhsT=w_codes[:].bitcast(E4M3X4), lhsT_scale=w_scales[:],
+                                rhs=tab_wg[i][:].bitcast(E2M1X4), rhs_scale=tab_sg[:, cols[i]], start=True, stop=True)
         dtab_sg = sb.tile([P, J], U8, name="dtab_sg", align_bytes=64)
         nc.vector.tensor_copy(dtab_sg[:], dtab_s[:].indirect(offsets[:]))
-        dtab_wg = sb.tile([P, J], U16, name="dtab_wg", align_bytes=64)
+        dtab_wg = sb.tile([P, J], U16, name="dtab_wg", tag="c", align_bytes=64)
         nc.vector.tensor_copy(dtab_wg[:], dtab_w[:].indirect(offsets[:]))
         ta = ps.tile([P, J], F32, name="ta")
         nc.tensor.matmul_mx(out=ta[:], lhsT=w_codes[:].bitcast(E4M3X4), lhsT_scale=w_scales[:],
                             rhs=dtab_wg[:].bitcast(E2M1X4), rhs_scale=dtab_sg[:], start=True, stop=True)
 
+        og_c = sb.tile([P, 1], F32, name="og_c", tag="b", align_bytes=64)
+        base_t = sb.tile([P, G], F32, name="base_t", tag="c", align_bytes=64)
+        nc.sync.dma_start(og_c[:], og)
+        nc.sync.dma_start(base_t[:], base)
         pp = sb.tile([P, J], F32, name="pp")
         p = pp[:]
-        ph_t = sb.tile([P, J], F32, name="ph_t", tag="a", align_bytes=64)
-        z_t = sb.tile([P, G], F32, name="z_t", tag="b", align_bytes=64)
-        ph = ph_t[:]
-        z = z_t[:]
+        late = sb.tile([P, 2 * G], F32, name="late", tag="a", align_bytes=64)
+        ph = sb.tile([P, J], F32, name="ph")
+        z = late[:, :G]
+        s2 = late[:, G:]
         h = sb.tile([P, J], F32, name="h")
-        hsq = sb.tile([P, J], F32, name="hsq")
-        nc.scalar.activation(p, a[:], ACT.Sigmoid, scale=steep_c[:])
-        nc.scalar.activation(h[:], a[:], ACT.Tanh)
-        nc.scalar.activation(hsq[:], h[:], ACT.Square)
+        for i in range(HALVES):
+            nc.scalar.activation(pp[:, cols[i]], a[i][:], ACT.Sigmoid, scale=steep_c[:])
+            nc.scalar.activation(h[:, cols[i]], a[i][:], ACT.Tanh)
 
-        s2 = sb.tile([P, G], F32, name="s2")
         rz = sb.tile([P, G], F32, name="rz")
         m = sb.tile([P, G], F32, name="m")
-        JH, GH = J // HALVES, G // HALVES
-        cols = [slice(i * JH, (i + 1) * JH) for i in range(HALVES)]
-        gs = [slice(i * GH, (i + 1) * GH) for i in range(HALVES)]
         pt = [sb.tile([P, JH], F32, name=f"pt{i}") for i in range(HALVES)]
         d = [sb.tile([P, JH], F32, name=f"d{i}") for i in range(HALVES)]
         e = [sb.tile([P, JH], F32, name=f"e{i}") for i in range(HALVES)]
@@ -105,12 +104,16 @@ def tile_attend_tgroupvote_kernel(tc, dtab_words, dtab_scales, tab_words, tab_sc
         r = [sb.tile([P, GH], F32, name=f"r{i}") for i in range(HALVES)]
         y0 = [sb.tile([P, GH], F32, name=f"y0{i}") for i in range(HALVES)]
         y = sb.tile([P, G], F32, name="y")
+        nc.gpsimd.tensor_tensor(ph[:], p, h[:], ALU.mult)
         nc.vector.tensor_reduce(z, grouped(p), AXIS.X, ALU.add)
-        nc.vector.tensor_tensor(ph, p, h[:], ALU.mult)
-        nc.vector.reciprocal(rz[:], z)
-        nc.vector.tensor_reduce(s2[:], grouped(ph), AXIS.X, ALU.add)
+        rs = sb.tile([P, G], F32, name="rs", tag="r")
+        nc.scalar.activation(rs[:], z, ACT.Abs_reciprocal_sqrt)
+        nc.scalar.activation(rz[:], rs[:], ACT.Square)
+        hsq = sb.tile([P, J], F32, name="hsq", tag="r")
+        nc.scalar.activation(hsq[:], h[:], ACT.Square)
+        nc.vector.tensor_reduce(s2, grouped(ph[:]), AXIS.X, ALU.add)
         nc.vector.tensor_tensor(pt[0][:], ta[:, cols[0]], pp[:, cols[0]], ALU.mult)
-        nc.vector.tensor_tensor(m[:], s2[:], rz[:], ALU.mult)
+        nc.vector.tensor_tensor(m[:], s2, rz[:], ALU.mult)
         nc.vector.tensor_tensor(pt[1][:], ta[:, cols[1]], pp[:, cols[1]], ALU.mult)
         for i in range(HALVES):
             nc.vector.tensor_tensor(grouped(d[i][:]), grouped(h[:, cols[i]]), m[:, gs[i]].unsqueeze(2).to_broadcast([P, GH, GROUP]), ALU.subtract)

@@ -6,7 +6,12 @@ K, R, T, J, G = 512, 128, 2048, 512, 64
 GROUP = J // G
 P = 128
 PACK = 4
+QUADRANTS = 4
+LIST_ROWS = 16
 HALVES = 2
+JH, GH = J // HALVES, G // HALVES
+TERM_PITCH = 16
+BLOCK_WORDS = 8
 
 F32 = mybir.dt.float32
 BF16 = mybir.dt.bfloat16
@@ -27,106 +32,132 @@ def grouped(ap):
     return ap.rearrange("p (g i) -> p g i", i=GROUP)
 
 
+def load_scale_rows(nc, window, scales):
+    for q in range(QUADRANTS):
+        nc.sync.dma_start(window[32 * q : 32 * q + 4, :].bitcast(I32), scales[0, 4 * q : 4 * q + 4, :].bitcast(I32))
+
+
 def tile_attend_tgroupvote_kernel(tc, dtab_words, dtab_scales, tab_words, tab_scales, w1, steep, og, base, offs, out):
     nc = tc.nc
+    slots = [slice(i * JH, (i + 1) * JH) for i in range(HALVES)]
+    groups = [slice(i * GH, (i + 1) * GH) for i in range(HALVES)]
+
     with ExitStack() as ctx:
         sb = ctx.enter_context(tc.tile_pool(name="sb", bufs=1))
         ps = ctx.enter_context(tc.psum_pool(name="ps", bufs=1))
 
-        offsets = sb.tile([P, J // 16], U16, name="offsets")
+        offsets = sb.tile([P, J // LIST_ROWS], U16, name="offsets")
         tab_w = sb.tile([P, T], U16, name="tab_w")
         tab_s = sb.tile([P, T], U8, name="tab_s")
-        dtab_s = sb.tile([P, T], U8, name="dtab_s", tag="b", align_bytes=64)
+        dtab_s = sb.tile([P, T], U8, name="dtab_s", tag="after_dtab_s", align_bytes=64)
         w_raw = sb.tile([P, PACK, R], F32, name="w_raw")
-        dtab_w = sb.tile([P, T], U16, name="dtab_w", tag="a", align_bytes=64)
-        steep_c = sb.tile([P, 1], F32, name="steep_c")
+        dtab_w = sb.tile([P, T], U16, name="dtab_w", tag="after_dtab_w", align_bytes=64)
+        steep_col = sb.tile([P, 1], F32, name="steep_col")
 
         nc.vector.memset(tab_s[:].bitcast(I32), 0)
         nc.vector.memset(dtab_s[:].bitcast(I32), 0)
 
         nc.sync.dma_start(w_raw[:], w1.rearrange("(p t) r -> p t r", t=PACK))
         nc.sync.dma_start(offsets[:], offs)
-        nc.scalar.dma_start(steep_c[:], steep)
-        for q in range(4):
-            nc.sync.dma_start(tab_s[32 * q : 32 * q + 4, :].bitcast(I32), tab_scales[0, 4 * q : 4 * q + 4, :].bitcast(I32))
+        nc.scalar.dma_start(steep_col[:], steep)
+        load_scale_rows(nc, tab_s, tab_scales)
         nc.sync.dma_start(tab_w[:].bitcast(I32), tab_words[0].bitcast(I32))
-        for q in range(4):
-            nc.sync.dma_start(dtab_s[32 * q : 32 * q + 4, :].bitcast(I32), dtab_scales[0, 4 * q : 4 * q + 4, :].bitcast(I32))
+        load_scale_rows(nc, dtab_s, dtab_scales)
         nc.sync.dma_start(dtab_w[:].bitcast(I32), dtab_words[0].bitcast(I32))
 
         w_bf = sb.tile([P, R, PACK], BF16, name="w_bf", align_bytes=64)
         w_codes = sb.tile([P, R], U32, name="w_codes", align_bytes=64)
         w_scales = sb.tile([P, R], U8, name="w_scales", align_bytes=64)
-        tab_wg = [sb.tile([P, J // HALVES], U16, name=f"tab_wg{i}", align_bytes=64) for i in range(HALVES)]
-        tab_sg = sb.tile([P, J], U8, name="tab_sg", align_bytes=64)
+        tab_w_listed = [sb.tile([P, JH], U16, name=f"tab_w_listed{i}", align_bytes=64) for i in range(HALVES)]
+        tab_s_listed = sb.tile([P, J], U8, name="tab_s_listed", align_bytes=64)
 
         nc.vector.tensor_copy(w_bf[:], w_raw[:].rearrange("p t r -> p r t"))
-        nc.vector.tensor_copy(tab_sg[:], tab_s[:].indirect(offsets[:]))
+        nc.vector.tensor_copy(tab_s_listed[:], tab_s[:].indirect(offsets[:]))
         nc.vector.quantize_mx(out=w_codes[:].bitcast(E4M3X4), scales=w_scales[:], in_=w_bf[:].rearrange("p r t -> p (r t)"))
-        JH, GH = J // HALVES, G // HALVES
-        cols = [slice(i * JH, (i + 1) * JH) for i in range(HALVES)]
-        gs = [slice(i * GH, (i + 1) * GH) for i in range(HALVES)]
+
         a = [ps.tile([P, JH], F32, name=f"a{i}") for i in range(HALVES)]
         for i in range(HALVES):
-            nc.vector.tensor_copy(tab_wg[i][:], tab_w[:].indirect(offsets[:, i * JH // 16 : (i + 1) * JH // 16]))
-            nc.tensor.matmul_mx(out=a[i][:], lhsT=w_codes[:].bitcast(E4M3X4), lhsT_scale=w_scales[:],
-                                rhs=tab_wg[i][:].bitcast(E2M1X4), rhs_scale=tab_sg[:, cols[i]], start=True, stop=True)
-        dtab_sg = sb.tile([P, J], U8, name="dtab_sg", align_bytes=64)
-        nc.vector.tensor_copy(dtab_sg[:], dtab_s[:].indirect(offsets[:]))
-        dtab_wg = sb.tile([P, J], U16, name="dtab_wg", tag="c", align_bytes=64)
-        nc.vector.tensor_copy(dtab_wg[:], dtab_w[:].indirect(offsets[:]))
-        ta = ps.tile([P, J], F32, name="ta")
-        nc.tensor.matmul_mx(out=ta[:], lhsT=w_codes[:].bitcast(E4M3X4), lhsT_scale=w_scales[:],
-                            rhs=dtab_wg[:].bitcast(E2M1X4), rhs_scale=dtab_sg[:], start=True, stop=True)
+            half_list = offsets[:, i * JH // LIST_ROWS : (i + 1) * JH // LIST_ROWS]
+            nc.vector.tensor_copy(tab_w_listed[i][:], tab_w[:].indirect(half_list))
+            nc.tensor.matmul_mx(
+                out=a[i][:],
+                lhsT=w_codes[:].bitcast(E4M3X4),
+                lhsT_scale=w_scales[:],
+                rhs=tab_w_listed[i][:].bitcast(E2M1X4),
+                rhs_scale=tab_s_listed[:, slots[i]],
+                start=True,
+                stop=True,
+            )
 
-        og_c = sb.tile([P, 1], F32, name="og_c", tag="b", align_bytes=64)
-        base_t = sb.tile([P, G], F32, name="base_t", tag="c", align_bytes=64)
-        nc.sync.dma_start(og_c[:], og)
-        nc.sync.dma_start(base_t[:], base)
-        pp = sb.tile([P, J], F32, name="pp")
-        p = pp[:]
-        late = sb.tile([P, 2 * G], F32, name="late", tag="a", align_bytes=64)
+        dtab_s_listed = sb.tile([P, J], U8, name="dtab_s_listed", align_bytes=64)
+        nc.vector.tensor_copy(dtab_s_listed[:], dtab_s[:].indirect(offsets[:]))
+        dtab_w_listed = sb.tile([P, J], U16, name="dtab_w_listed", align_bytes=64)
+        nc.vector.tensor_copy(dtab_w_listed[:], dtab_w[:].indirect(offsets[:]))
+        ta = ps.tile([P, J], F32, name="ta")
+        nc.tensor.matmul_mx(
+            out=ta[:],
+            lhsT=w_codes[:].bitcast(E4M3X4),
+            lhsT_scale=w_scales[:],
+            rhs=dtab_w_listed[:].bitcast(E2M1X4),
+            rhs_scale=dtab_s_listed[:],
+            start=True,
+            stop=True,
+        )
+
+        og_base = sb.tile([P, BLOCK_WORDS + G], F32, name="og_base", tag="after_dtab_s", align_bytes=64)
+        og_col = og_base[:, 0:1]
+        base_rows = og_base[:, BLOCK_WORDS:]
+        nc.sync.dma_start(og_col, og)
+        nc.sync.dma_start(base_rows, base)
+
+        p = sb.tile([P, J], F32, name="p")
+        sums = sb.tile([P, 2 * G], F32, name="sums", tag="after_dtab_w", align_bytes=64)
         ph = sb.tile([P, J], F32, name="ph")
-        z = late[:, :G]
-        s2 = late[:, G:]
+        neg_z = sums[:, :G]
+        sum_ph = sums[:, G:]
         h = sb.tile([P, J], F32, name="h")
         for i in range(HALVES):
-            nc.scalar.activation(pp[:, cols[i]], a[i][:], ACT.Sigmoid, scale=steep_c[:])
-            nc.scalar.activation(h[:, cols[i]], a[i][:], ACT.Tanh)
+            nc.scalar.activation(p[:, slots[i]], a[i][:], ACT.Sigmoid, scale=steep_col[:])
+            nc.scalar.activation(h[:, slots[i]], a[i][:], ACT.Tanh)
 
-        rz = sb.tile([P, G], F32, name="rz")
+        inv_z = sb.tile([P, G], F32, name="inv_z")
         m = sb.tile([P, G], F32, name="m")
-        pt = [sb.tile([P, JH], F32, name=f"pt{i}") for i in range(HALVES)]
-        d = [sb.tile([P, JH], F32, name=f"d{i}") for i in range(HALVES)]
-        e = [sb.tile([P, JH], F32, name=f"e{i}") for i in range(HALVES)]
-        f = [sb.tile([P, JH], F32, name=f"f{i}") for i in range(HALVES)]
-        t = [sb.tile([P, JH], F32, name=f"t{i}") for i in range(HALVES)]
-        r = [sb.tile([P, GH], F32, name=f"r{i}") for i in range(HALVES)]
-        y0 = [sb.tile([P, GH], F32, name=f"y0{i}") for i in range(HALVES)]
+        gain = [sb.tile([P, JH], F32, name=f"gain{i}") for i in range(HALVES)]
+        centred = [sb.tile([P, JH], F32, name=f"centred{i}") for i in range(HALVES)]
+        pull = [sb.tile([P, JH], F32, name=f"pull{i}") for i in range(HALVES)]
+        rest = [sb.tile([P, JH], F32, name=f"rest{i}") for i in range(HALVES)]
+        terms = sb.tile([P, G, TERM_PITCH], F32, name="terms", align_bytes=64)
+        totals = [sb.tile([P, GH], F32, name=f"totals{i}") for i in range(HALVES)]
         y = sb.tile([P, G], F32, name="y")
-        nc.gpsimd.tensor_tensor(ph[:], p, h[:], ALU.mult)
-        nc.vector.tensor_reduce(z, grouped(p), AXIS.X, ALU.add)
-        rs = sb.tile([P, G], F32, name="rs", tag="r")
-        nc.scalar.activation(rs[:], z, ACT.Abs_reciprocal_sqrt)
-        nc.scalar.activation(rz[:], rs[:], ACT.Square)
-        hsq = sb.tile([P, J], F32, name="hsq", tag="r")
-        nc.scalar.activation(hsq[:], h[:], ACT.Square)
-        nc.vector.tensor_reduce(s2, grouped(ph[:]), AXIS.X, ALU.add)
-        nc.vector.tensor_tensor(pt[0][:], ta[:, cols[0]], pp[:, cols[0]], ALU.mult)
-        nc.vector.tensor_tensor(m[:], s2, rz[:], ALU.mult)
-        nc.vector.tensor_tensor(pt[1][:], ta[:, cols[1]], pp[:, cols[1]], ALU.mult)
+
+        nc.gpsimd.tensor_tensor(ph[:], p[:], h[:], ALU.mult)
+        nc.vector.tensor_reduce(neg_z, grouped(p[:]), AXIS.X, ALU.add, negate=True)
+        nc.gpsimd.tensor_tensor(terms[:, :, GROUP], base_rows, neg_z, ALU.mult)
+
+        inv_root = sb.tile([P, G], F32, name="inv_root", tag="after_inv_root")
+        nc.scalar.activation(inv_root[:], neg_z, ACT.Abs_reciprocal_sqrt)
+        nc.scalar.activation(inv_z[:], inv_root[:], ACT.Square)
+        h_sq = sb.tile([P, J], F32, name="h_sq", tag="after_inv_root")
+        nc.scalar.activation(h_sq[:], h[:], ACT.Square)
+
+        nc.vector.tensor_reduce(sum_ph, grouped(ph[:]), AXIS.X, ALU.add)
+        nc.vector.scalar_tensor_tensor(gain[0][:], ta[:, slots[0]], og_col, p[:, slots[0]], ALU.mult, ALU.mult)
+        nc.vector.tensor_tensor(m[:], sum_ph, inv_z[:], ALU.mult)
+        nc.vector.scalar_tensor_tensor(gain[1][:], ta[:, slots[1]], og_col, p[:, slots[1]], ALU.mult, ALU.mult)
+
         for i in range(HALVES):
-            nc.vector.tensor_tensor(grouped(d[i][:]), grouped(h[:, cols[i]]), m[:, gs[i]].unsqueeze(2).to_broadcast([P, GH, GROUP]), ALU.subtract)
+            m_by_slot = m[:, groups[i]].unsqueeze(2).to_broadcast([P, GH, GROUP])
+            nc.vector.tensor_tensor(grouped(centred[i][:]), grouped(h[:, slots[i]]), m_by_slot, ALU.subtract)
         for i in range(HALVES):
-            nc.vector.scalar_tensor_tensor(e[i][:], pp[:, cols[i]], 1.0, d[i][:], ALU.subtract, ALU.mult)
+            nc.vector.scalar_tensor_tensor(pull[i][:], p[:, slots[i]], 1.0, centred[i][:], ALU.subtract, ALU.mult)
         for i in range(HALVES):
-            nc.vector.scalar_tensor_tensor(f[i][:], e[i][:], steep_c[:], hsq[:, cols[i]], ALU.mult, ALU.add)
+            nc.vector.scalar_tensor_tensor(rest[i][:], pull[i][:], steep_col[:], h_sq[:, slots[i]], ALU.mult, ALU.add)
         for i in range(HALVES):
-            nc.vector.scalar_tensor_tensor(t[i][:], f[i][:], 1.0, pt[i][:], ALU.subtract, ALU.mult)
+            nc.vector.scalar_tensor_tensor(
+                terms[:, groups[i], :GROUP], grouped(rest[i][:]), 1.0, grouped(gain[i][:]), ALU.subtract, ALU.mult
+            )
         for i in range(HALVES):
-            nc.vector.tensor_reduce(r[i][:], grouped(t[i][:]), AXIS.X, ALU.add)
+            nc.vector.tensor_reduce(totals[i][:], terms[:, groups[i], : GROUP + 1], AXIS.X, ALU.add)
         for i in range(HALVES):
-            nc.vector.scalar_tensor_tensor(y0[i][:], r[i][:], og_c[:], rz[:, gs[i]], ALU.mult, ALU.mult)
-        for i in range(HALVES):
-            nc.vector.tensor_tensor(y[:, gs[i]], base_t[:, gs[i]], y0[i][:], ALU.subtract)
+            nc.vector.scalar_tensor_tensor(y[:, groups[i]], totals[i][:], -1.0, inv_z[:, groups[i]], ALU.mult, ALU.mult)
         nc.sync.dma_start(out, y[:])

from contextlib import ExitStack

import concourse.mybir as mybir

K, R, T, J, G = 512, 128, 2048, 512, 64
GROUP = J // G
P = 128
PACK = 4
QUADRANTS = 4
LIST_ROWS = 16
HALVES = 2
JH, GH = J // HALVES, G // HALVES
TERM_PITCH = 16
BLOCK_WORDS = 8

F32 = mybir.dt.float32
BF16 = mybir.dt.bfloat16
I32 = mybir.dt.int32
U32 = mybir.dt.uint32
U16 = mybir.dt.uint16
U8 = mybir.dt.uint8
E4M3X4 = mybir.dt.float8_e4m3fn_x4
E2M1X4 = mybir.dt.float4_e2m1fn_x4
ALU = mybir.AluOpType
ACT = mybir.ActivationFunctionType
AXIS = mybir.AxisListType

FLOPS = 2 * 2 * K * R * J


def grouped(ap):
    return ap.rearrange("p (g i) -> p g i", i=GROUP)


def load_scale_rows(nc, window, scales):
    for q in range(QUADRANTS):
        nc.sync.dma_start(window[32 * q : 32 * q + 4, :].bitcast(I32), scales[0, 4 * q : 4 * q + 4, :].bitcast(I32))


def tile_attend_tgroupvote_kernel(tc, dtab_words, dtab_scales, tab_words, tab_scales, w1, steep, og, base, offs, out):
    nc = tc.nc
    slots = [slice(i * JH, (i + 1) * JH) for i in range(HALVES)]
    groups = [slice(i * GH, (i + 1) * GH) for i in range(HALVES)]

    with ExitStack() as ctx:
        sb = ctx.enter_context(tc.tile_pool(name="sb", bufs=1))
        ps = ctx.enter_context(tc.psum_pool(name="ps", bufs=1))

        offsets = sb.tile([P, J // LIST_ROWS], U16, name="offsets")
        tab_w = sb.tile([P, T], U16, name="tab_w")
        tab_s = sb.tile([P, T], U8, name="tab_s")
        dtab_s = sb.tile([P, T], U8, name="dtab_s", tag="after_dtab_s", align_bytes=64)
        w_raw = sb.tile([P, PACK, R], F32, name="w_raw")
        dtab_w = sb.tile([P, T], U16, name="dtab_w", tag="after_dtab_w", align_bytes=64)
        steep_col = sb.tile([P, 1], F32, name="steep_col")

        nc.vector.memset(tab_s[:].bitcast(I32), 0)
        nc.vector.memset(dtab_s[:].bitcast(I32), 0)

        nc.sync.dma_start(w_raw[:], w1.rearrange("(p t) r -> p t r", t=PACK))
        nc.sync.dma_start(offsets[:], offs)
        nc.scalar.dma_start(steep_col[:], steep)
        load_scale_rows(nc, tab_s, tab_scales)
        nc.sync.dma_start(tab_w[:].bitcast(I32), tab_words[0].bitcast(I32))
        load_scale_rows(nc, dtab_s, dtab_scales)
        nc.sync.dma_start(dtab_w[:].bitcast(I32), dtab_words[0].bitcast(I32))

        w_bf = sb.tile([P, R, PACK], BF16, name="w_bf", align_bytes=64)
        w_codes = sb.tile([P, R], U32, name="w_codes", align_bytes=64)
        w_scales = sb.tile([P, R], U8, name="w_scales", align_bytes=64)
        tab_w_listed = [sb.tile([P, JH], U16, name=f"tab_w_listed{i}", align_bytes=64) for i in range(HALVES)]
        tab_s_listed = sb.tile([P, J], U8, name="tab_s_listed", align_bytes=64)

        nc.vector.tensor_copy(w_bf[:], w_raw[:].rearrange("p t r -> p r t"))
        nc.vector.tensor_copy(tab_s_listed[:], tab_s[:].indirect(offsets[:]))
        nc.vector.quantize_mx(out=w_codes[:].bitcast(E4M3X4), scales=w_scales[:], in_=w_bf[:].rearrange("p r t -> p (r t)"))

        a = [ps.tile([P, JH], F32, name=f"a{i}") for i in range(HALVES)]
        for i in range(HALVES):
            half_list = offsets[:, i * JH // LIST_ROWS : (i + 1) * JH // LIST_ROWS]
            nc.vector.tensor_copy(tab_w_listed[i][:], tab_w[:].indirect(half_list))
            nc.tensor.matmul_mx(
                out=a[i][:],
                lhsT=w_codes[:].bitcast(E4M3X4),
                lhsT_scale=w_scales[:],
                rhs=tab_w_listed[i][:].bitcast(E2M1X4),
                rhs_scale=tab_s_listed[:, slots[i]],
                start=True,
                stop=True,
            )

        dtab_s_listed = sb.tile([P, J], U8, name="dtab_s_listed", align_bytes=64)
        nc.vector.tensor_copy(dtab_s_listed[:], dtab_s[:].indirect(offsets[:]))
        dtab_w_listed = sb.tile([P, J], U16, name="dtab_w_listed", align_bytes=64)
        nc.vector.tensor_copy(dtab_w_listed[:], dtab_w[:].indirect(offsets[:]))
        ta = ps.tile([P, J], F32, name="ta")
        nc.tensor.matmul_mx(
            out=ta[:],
            lhsT=w_codes[:].bitcast(E4M3X4),
            lhsT_scale=w_scales[:],
            rhs=dtab_w_listed[:].bitcast(E2M1X4),
            rhs_scale=dtab_s_listed[:],
            start=True,
            stop=True,
        )

        og_base = sb.tile([P, BLOCK_WORDS + G], F32, name="og_base", tag="after_dtab_s", align_bytes=64)
        og_col = og_base[:, 0:1]
        base_rows = og_base[:, BLOCK_WORDS:]
        nc.sync.dma_start(og_col, og)
        nc.sync.dma_start(base_rows, base)

        p = sb.tile([P, J], F32, name="p")
        sums = sb.tile([P, 2 * G], F32, name="sums", tag="after_dtab_w", align_bytes=64)
        ph = sb.tile([P, J], F32, name="ph")
        neg_z = sums[:, :G]
        sum_ph = sums[:, G:]
        h = sb.tile([P, J], F32, name="h")
        for i in range(HALVES):
            nc.scalar.activation(p[:, slots[i]], a[i][:], ACT.Sigmoid, scale=steep_col[:])
            nc.scalar.activation(h[:, slots[i]], a[i][:], ACT.Tanh)

        inv_z = sb.tile([P, G], F32, name="inv_z")
        m = sb.tile([P, G], F32, name="m")
        gain = [sb.tile([P, JH], F32, name=f"gain{i}") for i in range(HALVES)]
        centred = [sb.tile([P, JH], F32, name=f"centred{i}") for i in range(HALVES)]
        pull = [sb.tile([P, JH], F32, name=f"pull{i}") for i in range(HALVES)]
        rest = [sb.tile([P, JH], F32, name=f"rest{i}") for i in range(HALVES)]
        terms = sb.tile([P, G, TERM_PITCH], F32, name="terms", align_bytes=64)
        totals = [sb.tile([P, GH], F32, name=f"totals{i}") for i in range(HALVES)]
        y = sb.tile([P, G], F32, name="y")

        nc.gpsimd.tensor_tensor(ph[:], p[:], h[:], ALU.mult)
        nc.vector.tensor_reduce(neg_z, grouped(p[:]), AXIS.X, ALU.add, negate=True)
        nc.gpsimd.tensor_tensor(terms[:, :, GROUP], base_rows, neg_z, ALU.mult)

        inv_root = sb.tile([P, G], F32, name="inv_root", tag="after_inv_root")
        nc.scalar.activation(inv_root[:], neg_z, ACT.Abs_reciprocal_sqrt)
        nc.scalar.activation(inv_z[:], inv_root[:], ACT.Square)
        h_sq = sb.tile([P, J], F32, name="h_sq", tag="after_inv_root")
        nc.scalar.activation(h_sq[:], h[:], ACT.Square)

        nc.vector.tensor_reduce(sum_ph, grouped(ph[:]), AXIS.X, ALU.add)
        nc.vector.scalar_tensor_tensor(gain[0][:], ta[:, slots[0]], og_col, p[:, slots[0]], ALU.mult, ALU.mult)
        nc.vector.tensor_tensor(m[:], sum_ph, inv_z[:], ALU.mult)
        nc.vector.scalar_tensor_tensor(gain[1][:], ta[:, slots[1]], og_col, p[:, slots[1]], ALU.mult, ALU.mult)

        for i in range(HALVES):
            m_by_slot = m[:, groups[i]].unsqueeze(2).to_broadcast([P, GH, GROUP])
            nc.vector.tensor_tensor(grouped(centred[i][:]), grouped(h[:, slots[i]]), m_by_slot, ALU.subtract)
        for i in range(HALVES):
            nc.vector.scalar_tensor_tensor(pull[i][:], p[:, slots[i]], 1.0, centred[i][:], ALU.subtract, ALU.mult)
        for i in range(HALVES):
            nc.vector.scalar_tensor_tensor(rest[i][:], pull[i][:], steep_col[:], h_sq[:, slots[i]], ALU.mult, ALU.add)
        for i in range(HALVES):
            nc.vector.scalar_tensor_tensor(
                terms[:, groups[i], :GROUP], grouped(rest[i][:]), 1.0, grouped(gain[i][:]), ALU.subtract, ALU.mult
            )
        for i in range(HALVES):
            nc.vector.tensor_reduce(totals[i][:], terms[:, groups[i], : GROUP + 1], AXIS.X, ALU.add)
        for i in range(HALVES):
            nc.vector.scalar_tensor_tensor(y[:, groups[i]], totals[i][:], -1.0, inv_z[:, groups[i]], ALU.mult, ALU.mult)
        nc.sync.dma_start(out, y[:])
